import numpy as np
import ml_dtypes


def mxq(x, axis, fmt="e4m3"):
    dtype, down = {"e4m3": (ml_dtypes.float8_e4m3fn, 7), "e5m2": (ml_dtypes.float8_e5m2, 14)}[fmt]
    v = np.moveaxis(np.asarray(x, np.float32).astype(ml_dtypes.bfloat16).astype(np.float64), axis, -1)
    blocks = v.reshape(v.shape[:-1] + (-1, 32))
    amax = np.abs(blocks).max(-1, keepdims=True)
    byte = np.maximum(np.where(amax > 0, np.frexp(amax)[1] - 1 + 127, 0) - down, 1)
    scale = np.exp2(byte - 127.0)
    codes = (blocks / scale).astype(np.float32).astype(dtype).astype(np.float64)
    return np.moveaxis((codes * scale).reshape(v.shape), -1, axis)


WIDE = False


def mx_kscale(k):
    if not WIDE:
        return np.ones(k)
    levels = np.array([10, -10, 5, -5, 0])
    if k % 512:
        return np.exp2(np.random.permutation(np.resize(levels, k // 32))).repeat(32)
    a = np.empty((k // 512, 16))
    for p in range(k // 512):
        a[p, :8] = np.random.permutation(np.resize(levels, 8))
        for g in range(8):
            far = levels[np.abs(levels - a[p, g]) >= 10]
            a[p, g + 8] = far[np.random.randint(len(far))]
    return np.exp2(a.ravel()).repeat(32)


def f64(x):
    return np.asarray(x).astype(np.float64)


def striped(idx):
    return np.tile(idx.reshape(-1, 16).T, (8, 1)).astype(np.uint16)


def unstriped(offs):
    return offs[:16].T.reshape(-1).astype(np.int64)


E2M1 = np.array([0.0, 0.5, 1.0, 1.5, 2.0, 3.0, 4.0, 6.0, -0.0, -0.5, -1.0, -1.5, -2.0, -3.0, -4.0, -6.0])


def pack_weight(w, fmt):
    k, n = w.shape
    w = f64(np.asarray(w, np.float32).astype(ml_dtypes.bfloat16)).reshape(k // 32, 32, n)
    amax = np.abs(w).max(1)
    if fmt == "e4m3":
        byte = np.frexp(amax)[1] - 1 + 127 - 7
    else:
        mant, ex = np.frexp(amax / 6.0)
        byte = np.where(mant > 0.5, ex, ex - 1) + 127
    byte = np.clip(np.where(amax > 0, byte, 1), 1, 254)
    scaled = (w * np.exp2(127.0 - byte)[:, None, :]).reshape(k, n).astype(np.float32)
    by_word = np.ascontiguousarray(scaled.reshape(k // 512, 128, 4, n).transpose(0, 1, 3, 2))
    if fmt == "e4m3":
        words = by_word.astype(ml_dtypes.float8_e4m3fn).view(np.uint8)
    else:
        c = by_word.astype(ml_dtypes.float4_e2m1fn).view(np.uint8) & 0xF
        words = (c[..., 0::2] | (c[..., 1::2] << 4)).reshape(k // 512, 128, 2 * n)
    return np.ascontiguousarray(words), np.ascontiguousarray(byte.astype(np.uint8).reshape(k // 512, 16, n))


def unpack_weight(words, scales, fmt):
    g, _, n = scales.shape
    words = np.ascontiguousarray(words).reshape(g, 128, n, -1)
    if fmt == "e4m3":
        vals = words.view(ml_dtypes.float8_e4m3fn).astype(np.float64)
    else:
        nib = np.empty((g, 128, n, 4), np.uint8)
        nib[..., 0::2] = words & 0xF
        nib[..., 1::2] = words >> 4
        vals = E2M1[nib]
    vals = vals * np.repeat(np.exp2(scales.astype(np.float64) - 127.0), 8, axis=1)[..., None]
    return vals.transpose(0, 1, 3, 2).reshape(g * 512, n)


def gelu(v):
    return 0.5 * v * (1.0 + np.tanh(np.sqrt(2.0 / np.pi) * (v + 0.044715 * v**3)))


K, H, N, K2, T, T3, S, P = 1024, 1024, 512, 1536, 4096, 2048, 1024, 512

def setup_inputs():
    n = np.random.standard_normal
    s = mx_kscale(K)[:, None]
    s2 = mx_kscale(K2)[:, None]
    u = mx_kscale(H)[:, None]
    tab_words, tab_scales = pack_weight(n((K, T)) * s, "e4m3")
    tab2_words, tab2_scales = pack_weight(n((K2, T3)) * s2, "e4m3")
    w2_words, w2_scales = pack_weight(1.6 * n((H, N)) / np.sqrt(H) / u, "e2m1")
    w4_words, w4_scales = pack_weight(0.6 * n((K2, N)) / np.sqrt(K2) / s2, "e4m3")
    return {
        "tab_words": tab_words, "tab_scales": tab_scales,
        "offs": striped(np.random.permutation(T)[:S]),
        "tab2_words": tab2_words, "tab2_scales": tab2_scales,
        "offs2": striped(np.random.permutation(T3)[:P]),
        "pos1": striped(np.random.permutation(S)[:P]),
        "w1": (0.43 * n((K, H)) / np.sqrt(K) / s).astype(np.float32),
        "b1": np.random.uniform(-0.8, 0.8, H).astype(np.float32),
        "gain": (np.exp(0.3 * n(H)) * u[:, 0]).astype(np.float32),
        "w2_words": w2_words, "w2_scales": w2_scales,
        "w3": (1.6 * n((H, N)) / np.sqrt(H) / u).astype(np.float32),
        "w4_words": w4_words, "w4_scales": w4_scales,
    }

def reference(tab_words, tab_scales, offs, tab2_words, tab2_scales, offs2, pos1,
              w1, b1, gain, w2_words, w2_scales, w3, w4_words, w4_scales):
    v = unpack_weight(tab_words, tab_scales, "e4m3")[:, unstriped(offs)]
    v2 = unpack_weight(tab2_words, tab2_scales, "e4m3")[:, unstriped(offs2)]
    w2 = unpack_weight(w2_words, w2_scales, "e2m1")
    w4 = unpack_weight(w4_words, w4_scales, "e4m3")
    x = (mxq(f64(w1), 0, "e4m3").T @ v) + f64(b1)[:, None]
    h = np.sin(x) * f64(gain)[:, None]
    hq = mxq(h, 0, "e4m3")
    y2 = w2.T @ hq
    y3 = mxq(f64(w3), 0, "e4m3").T @ hq
    y = np.minimum(y2, y3)
    b = w4.T @ v2
    return y[:, unstriped(pos1)] * np.exp(b)

@@ -1,0 +1,259 @@
+from contextlib import ExitStack
+
+import concourse.mybir as mybir
+
+K, H, N, K2, T, T3, S, PICK = 1024, 1024, 512, 1536, 4096, 2048, 1024, 512
+FLOPS = 2 * (K * H * S + 2 * H * N * S + K2 * N * PICK)
+
+F32 = mybir.dt.float32
+BF16 = mybir.dt.bfloat16
+I32 = mybir.dt.int32
+U32 = mybir.dt.uint32
+U16 = mybir.dt.uint16
+U8 = mybir.dt.uint8
+FP8X4 = mybir.dt.float8_e4m3fn_x4
+FP4X4 = mybir.dt.float4_e2m1fn_x4
+ACT = mybir.ActivationFunctionType
+ALU = mybir.AluOpType
+
+P = 128
+PACK = 4
+PASS = P * PACK
+BANK = 512
+QUADS = 4
+QUAD = 32
+ROWS = 4
+LINE = 4
+SLOT = 8192
+
+
+def tile_list_patch_release_features_kernel(
+    tc, tab_words, tab_scales, offs, tab2_words, tab2_scales, offs2, pos1,
+    w1, b1, gain, w2_words, w2_scales, w3, w4_words, w4_scales, out,
+):
+    nc = tc.nc
+    k_passes, r_passes, m_passes = K // PASS, H // PASS, K2 // PASS
+    halves = S // BANK
+    n_tiles = N // P
+
+    with ExitStack() as ctx:
+        keep = ctx.enter_context(tc.tile_pool(name="keep", bufs=1))
+        ring = ctx.enter_context(tc.tile_pool(name="ring", bufs=1))
+        stage = ctx.enter_context(tc.tile_pool(name="stage", bufs=1))
+        psum = ctx.enter_context(tc.psum_pool(name="psum", bufs=8))
+
+        def kept(shape, dtype, name):
+            return keep.tile(shape, dtype, name=name, align_bytes=64)
+
+        idx = keep.tile([P, S // 16], U16, name="idx")
+        idx2 = keep.tile([P, PICK // 16], U16, name="idx2")
+        pick = keep.tile([P, PICK // 16], U16, name="pick")
+
+        tab_sc = kept([P, T], U8, "tab_sc")
+        tab2_sc = kept([P, T3], U8, "tab2_sc")
+        w2_sc = kept([P, r_passes, N], U8, "w2_sc")
+        w4_sc = kept([P, m_passes, N], U8, "w4_sc")
+        for plane in (tab_sc[:], tab2_sc[:], w2_sc[:], w4_sc[:]):
+            nc.vector.memset(plane.bitcast(I32), 0)
+        for plane, src, passes in ((tab_sc, tab_scales, k_passes), (tab2_sc, tab2_scales, m_passes)):
+            for q in range(QUADS):
+                nc.gpsimd.dma_start(
+                    out=plane[QUAD * q : QUAD * q + ROWS * passes, :].bitcast(I32),
+                    in_=src[:, ROWS * q : ROWS * (q + 1), :].bitcast(I32),
+                )
+        for plane, src in ((w2_sc, w2_scales), (w4_sc, w4_scales)):
+            for q in range(QUADS):
+                nc.gpsimd.dma_start(
+                    out=plane[QUAD * q : QUAD * q + ROWS, :, :].bitcast(I32),
+                    in_=src[:, ROWS * q : ROWS * (q + 1), :].rearrange("a r c -> r a c").bitcast(I32),
+                )
+
+        bias = kept([P, r_passes, PACK], F32, "bias")
+        gains = kept([P, r_passes, PACK], F32, "gains")
+        nc.scalar.dma_start(out=bias[:], in_=b1.rearrange("(b p t) -> p b t", p=P, t=PACK))
+        nc.scalar.dma_start(out=gains[:], in_=gain.rearrange("(b p t) -> p b t", p=P, t=PACK))
+
+        def staged(shape, dtype, name, slot):
+            return stage.tile(shape, dtype, name=name, align_bytes=64, offset=SLOT * slot)
+
+        def load_rows(src, name, slot):
+            raw = staged([P, PACK, BANK], F32, name, slot)
+            nc.sync.dma_start(out=raw[:], in_=src.rearrange("(p j) c -> p j c", j=PACK))
+            return raw
+
+        def load_words(src, width, name, slot):
+            words = staged([P, width], U32, name, slot)
+            nc.sync.dma_start(out=words[:].bitcast(I32), in_=src.rearrange("p t i -> p (t i)").bitcast(I32))
+            return words
+
+        def w1_block(a, b):
+            return w1[PASS * a : PASS * (a + 1), PASS * b : PASS * (b + 1)]
+
+        def quantize(grouped, name):
+            codes = kept([P, BANK], U32, name + "_codes")
+            scales = kept([P, BANK], U8, name + "_scales")
+            nc.vector.quantize_mx(out=codes[:].bitcast(FP8X4), scales=scales[:], in_=grouped[:])
+            return codes, scales
+
+        def new_grouped():
+            return ring.tile([P, BANK * PACK], BF16, name="grouped", bufs=3, align_bytes=64)
+
+        def round_w1(raw, copy, grouped):
+            copy(
+                out=grouped[:].rearrange("p (t m j) -> p m j t", t=PACK, j=PACK),
+                in_=raw[:].rearrange("p j (m t) -> p m j t", t=PACK),
+            )
+            return grouped
+
+        def round_w3(raw, copy):
+            grouped = new_grouped()
+            copy(
+                out=grouped[:].rearrange("p (c i j) -> p c j i", i=LINE, j=PACK),
+                in_=raw[:].rearrange("p j (c i) -> p c j i", i=LINE),
+            )
+            return grouped
+
+        def gather(window, offsets, dtype, name):
+            picked = kept([P, 16 * offsets.shape[1]], dtype, name)
+            nc.vector.tensor_copy(out=picked[:], in_=window[:].indirect(offsets))
+            return picked
+
+        def idx_half(j):
+            return idx[:, (BANK // 16) * j : (BANK // 16) * (j + 1)]
+
+        def mx(acc, lhs, lhs_sc, rhs, rhs_sc, step, steps):
+            nc.tensor.matmul_mx(
+                out=acc[:], lhsT=lhs, lhsT_scale=lhs_sc, rhs=rhs, rhs_scale=rhs_sc,
+                start=(step == 0), stop=(step == steps - 1),
+            )
+
+        def new_bank():
+            return psum.tile([P, BANK], F32, name="bank")
+
+        w1_raw = {}
+        w1_raw[0, 0] = load_rows(w1_block(0, 0), "w1_raw00", 0)
+        nc.sync.dma_start(out=idx[:], in_=offs)
+        w1_raw[1, 0] = load_rows(w1_block(1, 0), "w1_raw10", 2)
+        nc.sync.dma_start(out=idx2[:], in_=offs2)
+        tab = [load_words(tab_words[0], T, "tab0", 3)]
+        nc.sync.dma_start(out=pick[:], in_=pos1)
+
+        w1_q = {}
+        for a in range(k_passes):
+            w1_q[a, 0] = quantize(round_w1(w1_raw[a, 0], nc.scalar.copy, new_grouped()), "w1_%d0" % a)
+        v_sc = gather(tab_sc, idx[:], U8, "v_sc")
+
+        tab.append(load_words(tab_words[1], T, "tab1", 0))
+        w1_raw[0, 1] = load_rows(w1_block(0, 1), "w1_raw01", 2)
+
+        v = {}
+
+        def first_pass(acc, a, b, j, t):
+            codes, scales = w1_q[a, b]
+            cols = slice(P * t, P * (t + 1))
+            mx(acc, codes[:, cols].bitcast(FP8X4), scales[:, cols],
+               v[a, j][:].bitcast(FP8X4), v_sc[ROWS * a :, BANK * j : BANK * (j + 1)], a, k_passes)
+
+        def sines(banks, b):
+            sine = ring.tile([P, PACK, BANK], F32, name="sine", bufs=3)
+            for t in range(PACK):
+                nc.scalar.activation(out=sine[:, t, :], in_=banks[t][:], func=ACT.Sin, bias=bias[:, b, t : t + 1])
+            return sine
+
+        def features(sine, b):
+            grouped = new_grouped()
+            nc.vector.tensor_tensor(
+                out=grouped[:].rearrange("p (c i t) -> p c t i", i=LINE, t=PACK),
+                in0=sine[:].rearrange("p t (c i) -> p c t i", i=LINE),
+                in1=gains[:, b, :].unsqueeze(1).unsqueeze(3).to_broadcast([P, BANK // LINE, PACK, LINE]),
+                op=ALU.mult,
+            )
+            return grouped
+
+        banks = {}
+        for j in range(halves):
+            v[0, j] = gather(tab[0], idx_half(j), U32, "v0%d" % j)
+            banks[j] = [new_bank() for t in range(PACK)]
+            for t in range(PACK):
+                first_pass(banks[j][t], 0, 0, j, t)
+        v2_sc = gather(tab2_sc, idx2[:], U8, "v2_sc")
+        w1_raw[1, 1] = load_rows(w1_block(1, 1), "w1_raw11", 3)
+        w3_raw = [load_rows(w3[0:PASS, :], "w3_raw0", 4)]
+        sine = {}
+        for j in range(halves):
+            v[1, j] = gather(tab[1], idx_half(j), U32, "v1%d" % j)
+            for t in range(PACK):
+                first_pass(banks[j][t], 1, 0, j, t)
+            sine[0, j] = sines(banks[j], 0)
+
+        w3_raw.append(load_rows(w3[PASS : 2 * PASS, :], "w3_raw1", 0))
+        tab2 = [load_words(tab2_words[0], T3, "tab20", 1)]
+        h_q = {}
+        w1_q[0, 1] = quantize(round_w1(w1_raw[0, 1], nc.vector.tensor_copy, staged([P, BANK * PACK], BF16, "g01", 5)), "w1_01")
+        tab2.append(load_words(tab2_words[1], T3, "tab21", 2))
+        w2 = staged([P, r_passes, 2 * N], U8, "w2", 5)
+        nc.sync.dma_start(out=w2[:].bitcast(I32), in_=w2_words.rearrange("a p c -> p a c").bitcast(I32))
+        h00 = features(sine[0, 0], 0)
+        w1_g = round_w1(w1_raw[1, 1], nc.vector.tensor_copy, new_grouped())
+        tab2.append(load_words(tab2_words[2], T3, "tab22", 3))
+        h_q[0, 0] = quantize(h00, "h00")
+        w1_q[1, 1] = quantize(w1_g, "w1_11")
+        for j in range(halves):
+            banks[j] = [new_bank() for t in range(PACK)]
+            for t in range(PACK):
+                for a in range(k_passes):
+                    first_pass(banks[j][t], a, 1, j, t)
+        h01 = features(sine[0, 1], 0)
+        w3_g = [round_w3(w3_raw[0], nc.scalar.copy)]
+        w4 = staged([P, m_passes, N], U32, "w4", 4)
+        nc.sync.dma_start(out=w4[:].bitcast(I32), in_=w4_words.rearrange("a p c i -> p a (c i)").bitcast(I32))
+        for j in range(halves):
+            sine[1, j] = sines(banks[j], 1)
+        w3_q = [quantize(w3_g[0], "w3_0")]
+        h_q[0, 1] = quantize(h01, "h01")
+        h10 = features(sine[1, 0], 1)
+        w3_g.append(round_w3(w3_raw[1], nc.scalar.copy))
+        v2 = [gather(tab2[0], idx2[:], U32, "v20")]
+        h_q[1, 0] = quantize(h10, "h10")
+        h11 = features(sine[1, 1], 1)
+        w3_q.append(quantize(w3_g[1], "w3_1"))
+        h_q[1, 1] = quantize(h11, "h11")
+        for a in range(1, m_passes):
+            v2.append(gather(tab2[a], idx2[:], U32, "v2%d" % a))
+
+        y = [kept([P, S], F32, "y%d" % m) for m in range(n_tiles)]
+
+        def readouts(m, j):
+            cols = slice(P * m, P * (m + 1))
+            y2, y3 = new_bank(), new_bank()
+            for b in range(r_passes):
+                codes, scales = h_q[b, j]
+                mx(y2, w2[:, b, 2 * P * m : 2 * P * (m + 1)].bitcast(FP4X4), w2_sc[:, b, cols],
+                   codes[:].bitcast(FP8X4), scales[:], b, r_passes)
+            for b in range(r_passes):
+                codes, scales = h_q[b, j]
+                w_codes, w_scales = w3_q[b]
+                mx(y3, w_codes[:, cols].bitcast(FP8X4), w_scales[:, cols],
+                   codes[:].bitcast(FP8X4), scales[:], b, r_passes)
+            y2_sb = ring.tile([P, BANK], F32, name="y2_sb", bufs=3)
+            nc.scalar.copy(out=y2_sb[:], in_=y2[:])
+            nc.vector.tensor_tensor(out=y[m][:, BANK * j : BANK * (j + 1)], in0=y3[:], in1=y2_sb[:], op=ALU.min)
+
+        def growth(m):
+            cols = slice(P * m, P * (m + 1))
+            acc = new_bank()
+            for a in range(m_passes):
+                mx(acc, w4[:, a, cols].bitcast(FP8X4), w4_sc[:, a, cols],
+                   v2[a][:].bitcast(FP8X4), v2_sc[ROWS * a :, :], a, m_passes)
+            factor = kept([P, PICK], F32, "factor%d" % m)
+            nc.scalar.activation(out=factor[:], in_=acc[:], func=ACT.Exp)
+            return factor
+
+        for m in range(n_tiles):
+            readouts(m, 0)
+        for m in range(n_tiles):
+            readouts(m, 1)
+            factor = growth(m)
+            result = ring.tile([P, PICK], F32, name="result", bufs=4)
+            nc.vector.tensor_tensor(out=result[:], in0=y[m][:].indirect(pick[:]), in1=factor[:], op=ALU.mult)
+            nc.sync.dma_start(out=out[P * m : P * (m + 1), :], in_=result[:])

@@ -25,6 +25,7 @@ QUAD = 32
 ROWS = 4
 LINE = 4
 SLOT = 8192
+ON_VECTOR = 1
 
 
 def tile_list_patch_release_features_kernel(
@@ -49,11 +50,13 @@ def tile_list_patch_release_features_kernel(
         idx2 = keep.tile([P, PICK // 16], U16, name="idx2")
         pick = keep.tile([P, PICK // 16], U16, name="pick")
 
-        tab_sc = kept([P, T], U8, "tab_sc")
+        tab_sc = stage.tile([P, T], U8, name="tab_sc", align_bytes=64, offset=SLOT * 6)
         tab2_sc = kept([P, T3], U8, "tab2_sc")
         w2_sc = kept([P, r_passes, N], U8, "w2_sc")
         w4_sc = kept([P, m_passes, N], U8, "w4_sc")
-        for plane in (tab_sc[:], tab2_sc[:], w2_sc[:], w4_sc[:]):
+        nc.gpsimd.memset(tab_sc[:, : T // 2].bitcast(I32), 0)
+        nc.vector.memset(tab_sc[:, T // 2 :].bitcast(I32), 0)
+        for plane in (tab2_sc[:], w2_sc[:], w4_sc[:]):
             nc.vector.memset(plane.bitcast(I32), 0)
         for plane, src, passes in ((tab_sc, tab_scales, k_passes), (tab2_sc, tab2_scales, m_passes)):
             for q in range(QUADS):
@@ -132,15 +135,15 @@ def tile_list_patch_release_features_kernel(
 
         w1_raw = {}
         w1_raw[0, 0] = load_rows(w1_block(0, 0), "w1_raw00", 0)
-        nc.sync.dma_start(out=idx[:], in_=offs)
         w1_raw[1, 0] = load_rows(w1_block(1, 0), "w1_raw10", 2)
-        nc.sync.dma_start(out=idx2[:], in_=offs2)
         tab = [load_words(tab_words[0], T, "tab0", 3)]
+        nc.sync.dma_start(out=idx[:], in_=offs)
+        nc.sync.dma_start(out=idx2[:], in_=offs2)
         nc.sync.dma_start(out=pick[:], in_=pos1)
 
         w1_q = {}
-        for a in range(k_passes):
-            w1_q[a, 0] = quantize(round_w1(w1_raw[a, 0], nc.scalar.copy, new_grouped()), "w1_%d0" % a)
+        for a, grouped in enumerate((staged([P, BANK * PACK], BF16, "g00", 1), new_grouped())):
+            w1_q[a, 0] = quantize(round_w1(w1_raw[a, 0], nc.scalar.copy, grouped), "w1_%d0" % a)
         v_sc = gather(tab_sc, idx[:], U8, "v_sc")
 
         tab.append(load_words(tab_words[1], T, "tab1", 0))
@@ -156,17 +159,20 @@ def tile_list_patch_release_features_kernel(
 
         def sines(banks, b):
             sine = ring.tile([P, PACK, BANK], F32, name="sine", bufs=3)
+            rows = ring.tile([P, PACK, BANK], BF16, name="rows", bufs=3)
             for t in range(PACK):
                 nc.scalar.activation(out=sine[:, t, :], in_=banks[t][:], func=ACT.Sin, bias=bias[:, b, t : t + 1])
-            return sine
+            for t in range(ON_VECTOR, PACK):
+                nc.scalar.activation(out=rows[:, t, :], in_=sine[:, t, :], func=ACT.Copy, scale=gains[:, b, t : t + 1])
+            return sine, rows
 
-        def features(sine, b):
-            grouped = new_grouped()
-            nc.vector.tensor_tensor(
+        def features(sine_rows, b, grouped):
+            sine, rows = sine_rows
+            for t in range(ON_VECTOR):
+                nc.vector.tensor_scalar_mul(out=rows[:, t, :], in0=sine[:, t, :], scalar1=gains[:, b, t : t + 1])
+            nc.vector.tensor_copy(
                 out=grouped[:].rearrange("p (c i t) -> p c t i", i=LINE, t=PACK),
-                in0=sine[:].rearrange("p t (c i) -> p c t i", i=LINE),
-                in1=gains[:, b, :].unsqueeze(1).unsqueeze(3).to_broadcast([P, BANK // LINE, PACK, LINE]),
-                op=ALU.mult,
+                in_=rows[:].rearrange("p t (c i) -> p c t i", i=LINE),
             )
             return grouped
 
@@ -176,12 +182,12 @@ def tile_list_patch_release_features_kernel(
             banks[j] = [new_bank() for t in range(PACK)]
             for t in range(PACK):
                 first_pass(banks[j][t], 0, 0, j, t)
-        v2_sc = gather(tab2_sc, idx2[:], U8, "v2_sc")
         w1_raw[1, 1] = load_rows(w1_block(1, 1), "w1_raw11", 3)
         w3_raw = [load_rows(w3[0:PASS, :], "w3_raw0", 4)]
         sine = {}
         for j in range(halves):
-            v[1, j] = gather(tab[1], idx_half(j), U32, "v1%d" % j)
+            v[1, j] = stage.tile([P, BANK], U32, name="v1%d" % j, align_bytes=64, offset=SLOT * 6 + 4 * BANK * j)
+            nc.vector.tensor_copy(out=v[1, j][:], in_=tab[1][:].indirect(idx_half(j)))
             for t in range(PACK):
                 first_pass(banks[j][t], 1, 0, j, t)
             sine[0, j] = sines(banks[j], 0)
@@ -191,35 +197,37 @@ def tile_list_patch_release_features_kernel(
         h_q = {}
         w1_q[0, 1] = quantize(round_w1(w1_raw[0, 1], nc.vector.tensor_copy, staged([P, BANK * PACK], BF16, "g01", 5)), "w1_01")
         tab2.append(load_words(tab2_words[1], T3, "tab21", 2))
+        v2_sc = stage.tile([P, PICK], U8, name="v2_sc", align_bytes=64, offset=SLOT * 5 + 2048)
+        nc.vector.tensor_copy(out=v2_sc[:], in_=tab2_sc[:].indirect(idx2[:]))
         w2 = staged([P, r_passes, 2 * N], U8, "w2", 5)
         nc.sync.dma_start(out=w2[:].bitcast(I32), in_=w2_words.rearrange("a p c -> p a c").bitcast(I32))
-        h00 = features(sine[0, 0], 0)
-        w1_g = round_w1(w1_raw[1, 1], nc.vector.tensor_copy, new_grouped())
+        w1_g = round_w1(w1_raw[1, 1], nc.vector.tensor_copy, staged([P, BANK * PACK], BF16, "g11", 7))
         tab2.append(load_words(tab2_words[2], T3, "tab22", 3))
-        h_q[0, 0] = quantize(h00, "h00")
         w1_q[1, 1] = quantize(w1_g, "w1_11")
+        h00 = features(sine[0, 0], 0, staged([P, BANK * PACK], BF16, "gh00", 7))
+        w3_g = [round_w3(w3_raw[0], nc.vector.tensor_copy)]
+        h_q[0, 0] = quantize(h00, "h00")
+        w3_q = [quantize(w3_g[0], "w3_0")]
         for j in range(halves):
             banks[j] = [new_bank() for t in range(PACK)]
             for t in range(PACK):
                 for a in range(k_passes):
                     first_pass(banks[j][t], a, 1, j, t)
-        h01 = features(sine[0, 1], 0)
-        w3_g = [round_w3(w3_raw[0], nc.scalar.copy)]
+        h01 = features(sine[0, 1], 0, new_grouped())
+        w3_g.append(round_w3(w3_raw[1], nc.vector.tensor_copy))
         w4 = staged([P, m_passes, N], U32, "w4", 4)
         nc.sync.dma_start(out=w4[:].bitcast(I32), in_=w4_words.rearrange("a p c i -> p a (c i)").bitcast(I32))
         for j in range(halves):
             sine[1, j] = sines(banks[j], 1)
-        w3_q = [quantize(w3_g[0], "w3_0")]
         h_q[0, 1] = quantize(h01, "h01")
-        h10 = features(sine[1, 0], 1)
-        w3_g.append(round_w3(w3_raw[1], nc.scalar.copy))
+        w3_q.append(quantize(w3_g[1], "w3_1"))
+        h10 = features(sine[1, 0], 1, new_grouped())
         v2 = [gather(tab2[0], idx2[:], U32, "v20")]
         h_q[1, 0] = quantize(h10, "h10")
-        h11 = features(sine[1, 1], 1)
-        w3_q.append(quantize(w3_g[1], "w3_1"))
-        h_q[1, 1] = quantize(h11, "h11")
         for a in range(1, m_passes):
             v2.append(gather(tab2[a], idx2[:], U32, "v2%d" % a))
+        h11 = features(sine[1, 1], 1, stage.tile([P, BANK * PACK], BF16, name="gh11", align_bytes=64, offset=SLOT * 3 - 2048))
+        h_q[1, 1] = quantize(h11, "h11")
 
         y = [kept([P, S], F32, "y%d" % m) for m in range(n_tiles)]
 

@@ -25,7 +25,8 @@ QUAD = 32
 ROWS = 4
 LINE = 4
 SLOT = 8192
-ON_VECTOR = 1
+BANKS = 8
+ON_VECTOR = {(0, 0): 0, (0, 1): 0, (1, 0): 1, (1, 1): 1}
 
 
 def tile_list_patch_release_features_kernel(
@@ -41,7 +42,7 @@ def tile_list_patch_release_features_kernel(
         keep = ctx.enter_context(tc.tile_pool(name="keep", bufs=1))
         ring = ctx.enter_context(tc.tile_pool(name="ring", bufs=1))
         stage = ctx.enter_context(tc.tile_pool(name="stage", bufs=1))
-        psum = ctx.enter_context(tc.psum_pool(name="psum", bufs=8))
+        psum = ctx.enter_context(tc.psum_pool(name="psum", bufs=1))
 
         def kept(shape, dtype, name):
             return keep.tile(shape, dtype, name=name, align_bytes=64)
@@ -51,7 +52,7 @@ def tile_list_patch_release_features_kernel(
         pick = keep.tile([P, PICK // 16], U16, name="pick")
 
         tab_sc = stage.tile([P, T], U8, name="tab_sc", align_bytes=64, offset=SLOT * 6)
-        tab2_sc = kept([P, T3], U8, "tab2_sc")
+        tab2_sc = stage.tile([P, T3], U8, name="tab2_sc", align_bytes=64, offset=SLOT * 6 + T)
         w2_sc = kept([P, r_passes, N], U8, "w2_sc")
         w4_sc = kept([P, m_passes, N], U8, "w4_sc")
         nc.gpsimd.memset(tab_sc[:, : T // 2].bitcast(I32), 0)
@@ -71,13 +72,8 @@ def tile_list_patch_release_features_kernel(
                     in_=src[:, ROWS * q : ROWS * (q + 1), :].rearrange("a r c -> r a c").bitcast(I32),
                 )
 
-        bias = kept([P, r_passes, PACK], F32, "bias")
-        gains = kept([P, r_passes, PACK], F32, "gains")
-        nc.scalar.dma_start(out=bias[:], in_=b1.rearrange("(b p t) -> p b t", p=P, t=PACK))
-        nc.scalar.dma_start(out=gains[:], in_=gain.rearrange("(b p t) -> p b t", p=P, t=PACK))
-
-        def staged(shape, dtype, name, slot):
-            return stage.tile(shape, dtype, name=name, align_bytes=64, offset=SLOT * slot)
+        def staged(shape, dtype, name, slot, shift=0):
+            return stage.tile(shape, dtype, name=name, align_bytes=64, offset=SLOT * slot + shift)
 
         def load_rows(src, name, slot):
             raw = staged([P, PACK, BANK], F32, name, slot)
@@ -98,8 +94,8 @@ def tile_list_patch_release_features_kernel(
             nc.vector.quantize_mx(out=codes[:].bitcast(FP8X4), scales=scales[:], in_=grouped[:])
             return codes, scales
 
-        def new_grouped():
-            return ring.tile([P, BANK * PACK], BF16, name="grouped", bufs=3, align_bytes=64)
+        def new_rows():
+            return ring.tile([P, PACK, BANK], BF16, name="rows", bufs=3)
 
         def round_w1(raw, copy, grouped):
             copy(
@@ -108,8 +104,7 @@ def tile_list_patch_release_features_kernel(
             )
             return grouped
 
-        def round_w3(raw, copy):
-            grouped = new_grouped()
+        def round_w3(raw, copy, grouped):
             copy(
                 out=grouped[:].rearrange("p (c i j) -> p c j i", i=LINE, j=PACK),
                 in_=raw[:].rearrange("p j (c i) -> p c j i", i=LINE),
@@ -130,8 +125,8 @@ def tile_list_patch_release_features_kernel(
                 start=(step == 0), stop=(step == steps - 1),
             )
 
-        def new_bank():
-            return psum.tile([P, BANK], F32, name="bank")
+        def new_bank(n):
+            return psum.tile([P, BANK], F32, name="bank%d" % n)
 
         w1_raw = {}
         w1_raw[0, 0] = load_rows(w1_block(0, 0), "w1_raw00", 0)
@@ -142,14 +137,19 @@ def tile_list_patch_release_features_kernel(
         nc.sync.dma_start(out=pick[:], in_=pos1)
 
         w1_q = {}
-        for a, grouped in enumerate((staged([P, BANK * PACK], BF16, "g00", 1), new_grouped())):
+        for a, grouped in enumerate((staged([P, BANK * PACK], BF16, "g00", 1), staged([P, BANK * PACK], BF16, "g10", 8))):
             w1_q[a, 0] = quantize(round_w1(w1_raw[a, 0], nc.scalar.copy, grouped), "w1_%d0" % a)
         v_sc = gather(tab_sc, idx[:], U8, "v_sc")
 
         tab.append(load_words(tab_words[1], T, "tab1", 0))
         w1_raw[0, 1] = load_rows(w1_block(0, 1), "w1_raw01", 2)
 
+        bias = staged([P, r_passes, PACK], F32, "bias", 8, 512)
+        gains = staged([P, r_passes, PACK], F32, "gains", 8, 576)
+        nc.scalar.dma_start(out=bias[:], in_=b1.rearrange("(b p t) -> p b t", p=P, t=PACK))
+        nc.scalar.dma_start(out=gains[:], in_=gain.rearrange("(b p t) -> p b t", p=P, t=PACK))
         v = {}
+        tiles = {}
 
         def first_pass(acc, a, b, j, t):
             codes, scales = w1_q[a, b]
@@ -157,18 +157,17 @@ def tile_list_patch_release_features_kernel(
             mx(acc, codes[:, cols].bitcast(FP8X4), scales[:, cols],
                v[a, j][:].bitcast(FP8X4), v_sc[ROWS * a :, BANK * j : BANK * (j + 1)], a, k_passes)
 
-        def sines(banks, b):
+        def sines(banks, b, j, rows):
             sine = ring.tile([P, PACK, BANK], F32, name="sine", bufs=3)
-            rows = ring.tile([P, PACK, BANK], BF16, name="rows", bufs=3)
             for t in range(PACK):
                 nc.scalar.activation(out=sine[:, t, :], in_=banks[t][:], func=ACT.Sin, bias=bias[:, b, t : t + 1])
-            for t in range(ON_VECTOR, PACK):
+            for t in range(ON_VECTOR[b, j], PACK):
                 nc.scalar.activation(out=rows[:, t, :], in_=sine[:, t, :], func=ACT.Copy, scale=gains[:, b, t : t + 1])
             return sine, rows
 
-        def features(sine_rows, b, grouped):
-            sine, rows = sine_rows
-            for t in range(ON_VECTOR):
+        def features(b, j, grouped):
+            sine, rows = tiles[b, j]
+            for t in range(ON_VECTOR[b, j]):
                 nc.vector.tensor_scalar_mul(out=rows[:, t, :], in0=sine[:, t, :], scalar1=gains[:, b, t : t + 1])
             nc.vector.tensor_copy(
                 out=grouped[:].rearrange("p (c i t) -> p c t i", i=LINE, t=PACK),
@@ -179,61 +178,64 @@ def tile_list_patch_release_features_kernel(
         banks = {}
         for j in range(halves):
             v[0, j] = gather(tab[0], idx_half(j), U32, "v0%d" % j)
-            banks[j] = [new_bank() for t in range(PACK)]
+            banks[j] = [new_bank(PACK * j + t) for t in range(PACK)]
             for t in range(PACK):
                 first_pass(banks[j][t], 0, 0, j, t)
+        v2_sc = staged([P, PICK], U8, "v2_sc", 8)
+        nc.vector.tensor_copy(out=v2_sc[:], in_=tab2_sc[:].indirect(idx2[:]))
         w1_raw[1, 1] = load_rows(w1_block(1, 1), "w1_raw11", 3)
         w3_raw = [load_rows(w3[0:PASS, :], "w3_raw0", 4)]
-        sine = {}
         for j in range(halves):
-            v[1, j] = stage.tile([P, BANK], U32, name="v1%d" % j, align_bytes=64, offset=SLOT * 6 + 4 * BANK * j)
+            v[1, j] = stage.tile([P, BANK], U32, name="v1%d" % j, align_bytes=64, offset=SLOT * 6 + T * j)
             nc.vector.tensor_copy(out=v[1, j][:], in_=tab[1][:].indirect(idx_half(j)))
             for t in range(PACK):
                 first_pass(banks[j][t], 1, 0, j, t)
-            sine[0, j] = sines(banks[j], 0)
 
+        tiles[0, 0] = sines(banks[0], 0, 0, new_rows())
         w3_raw.append(load_rows(w3[PASS : 2 * PASS, :], "w3_raw1", 0))
         tab2 = [load_words(tab2_words[0], T3, "tab20", 1)]
         h_q = {}
         w1_q[0, 1] = quantize(round_w1(w1_raw[0, 1], nc.vector.tensor_copy, staged([P, BANK * PACK], BF16, "g01", 5)), "w1_01")
         tab2.append(load_words(tab2_words[1], T3, "tab21", 2))
-        v2_sc = stage.tile([P, PICK], U8, name="v2_sc", align_bytes=64, offset=SLOT * 5 + 2048)
-        nc.vector.tensor_copy(out=v2_sc[:], in_=tab2_sc[:].indirect(idx2[:]))
-        w2 = staged([P, r_passes, 2 * N], U8, "w2", 5)
-        nc.sync.dma_start(out=w2[:].bitcast(I32), in_=w2_words.rearrange("a p c -> p a c").bitcast(I32))
-        w1_g = round_w1(w1_raw[1, 1], nc.vector.tensor_copy, staged([P, BANK * PACK], BF16, "g11", 7))
+        w1_g = round_w1(w1_raw[1, 1], nc.vector.tensor_copy, staged([P, BANK * PACK], BF16, "g11", 7, 2048))
         tab2.append(load_words(tab2_words[2], T3, "tab22", 3))
         w1_q[1, 1] = quantize(w1_g, "w1_11")
-        h00 = features(sine[0, 0], 0, staged([P, BANK * PACK], BF16, "gh00", 7))
-        w3_g = [round_w3(w3_raw[0], nc.vector.tensor_copy)]
+        tiles[0, 1] = sines(banks[1], 0, 1, staged([P, PACK, BANK], BF16, "rows01", 7, 4096))
+        h00 = features(0, 0, staged([P, BANK * PACK], BF16, "gh00", 7))
+        w3_g = [round_w3(w3_raw[0], nc.vector.tensor_copy, staged([P, BANK * PACK], BF16, "g30", 10))]
         h_q[0, 0] = quantize(h00, "h00")
         w3_q = [quantize(w3_g[0], "w3_0")]
+        w2 = staged([P, r_passes, 2 * N], U8, "w2", 10)
+        nc.sync.dma_start(out=w2[:].bitcast(I32), in_=w2_words.rearrange("a p c -> p a c").bitcast(I32))
         for j in range(halves):
-            banks[j] = [new_bank() for t in range(PACK)]
+            banks[j] = [new_bank(PACK * j + t) for t in range(PACK)]
             for t in range(PACK):
                 for a in range(k_passes):
                     first_pass(banks[j][t], a, 1, j, t)
-        h01 = features(sine[0, 1], 0, new_grouped())
-        w3_g.append(round_w3(w3_raw[1], nc.vector.tensor_copy))
-        w4 = staged([P, m_passes, N], U32, "w4", 4)
-        nc.sync.dma_start(out=w4[:].bitcast(I32), in_=w4_words.rearrange("a p c i -> p a (c i)").bitcast(I32))
-        for j in range(halves):
-            sine[1, j] = sines(banks[j], 1)
-        h_q[0, 1] = quantize(h01, "h01")
+        w3_g.append(round_w3(w3_raw[1], nc.vector.tensor_copy, staged([P, BANK * PACK], BF16, "g31", 11)))
+        h01 = features(0, 1, staged([P, BANK * PACK], BF16, "gh01", 0))
         w3_q.append(quantize(w3_g[1], "w3_1"))
-        h10 = features(sine[1, 0], 1, new_grouped())
+        w4 = staged([P, m_passes, N], U32, "w4", 11)
+        nc.sync.dma_start(out=w4[:].bitcast(I32), in_=w4_words.rearrange("a p c i -> p a (c i)").bitcast(I32))
+        tiles[1, 0] = sines(banks[0], 1, 0, new_rows())
+        tiles[1, 1] = sines(banks[1], 1, 1, stage.tile([P, PACK, BANK], BF16, name="rows11", align_bytes=64, offset=SLOT * 9 + 2048))
         v2 = [gather(tab2[0], idx2[:], U32, "v20")]
+        h_q[0, 1] = quantize(h01, "h01")
+        v2.append(gather(tab2[1], idx2[:], U32, "v21"))
+        h10 = features(1, 0, staged([P, BANK * PACK], BF16, "gh10", 2, -2048))
         h_q[1, 0] = quantize(h10, "h10")
-        for a in range(1, m_passes):
-            v2.append(gather(tab2[a], idx2[:], U32, "v2%d" % a))
-        h11 = features(sine[1, 1], 1, stage.tile([P, BANK * PACK], BF16, name="gh11", align_bytes=64, offset=SLOT * 3 - 2048))
+        v2.append(staged([P, PICK], U32, "v22", 2, -2048))
+        nc.vector.tensor_copy(out=v2[2][:], in_=tab2[2][:].indirect(idx2[:]))
+        h11 = features(1, 1, stage.tile([P, BANK * PACK], BF16, name="gh11", align_bytes=64, offset=SLOT * 3 - 2048))
         h_q[1, 1] = quantize(h11, "h11")
 
-        y = [kept([P, S], F32, "y%d" % m) for m in range(n_tiles)]
+        y = [
+            stage.tile([P, S], F32, name="y%d" % m, align_bytes=64, offset=offset)
+            for m, offset in enumerate((SLOT * 3 - 4096, SLOT * 3, SLOT * 9, SLOT * 9 + 4096))
+        ]
 
-        def readouts(m, j):
+        def readouts(m, j, y2, y3):
             cols = slice(P * m, P * (m + 1))
-            y2, y3 = new_bank(), new_bank()
             for b in range(r_passes):
                 codes, scales = h_q[b, j]
                 mx(y2, w2[:, b, 2 * P * m : 2 * P * (m + 1)].bitcast(FP4X4), w2_sc[:, b, cols],
@@ -247,9 +249,8 @@ def tile_list_patch_release_features_kernel(
             nc.scalar.copy(out=y2_sb[:], in_=y2[:])
             nc.vector.tensor_tensor(out=y[m][:, BANK * j : BANK * (j + 1)], in0=y3[:], in1=y2_sb[:], op=ALU.min)
 
-        def growth(m):
+        def growth(m, acc):
             cols = slice(P * m, P * (m + 1))
-            acc = new_bank()
             for a in range(m_passes):
                 mx(acc, w4[:, a, cols].bitcast(FP8X4), w4_sc[:, a, cols],
                    v2[a][:].bitcast(FP8X4), v2_sc[ROWS * a :, :], a, m_passes)
@@ -258,10 +259,12 @@ def tile_list_patch_release_features_kernel(
             return factor
 
         for m in range(n_tiles):
-            readouts(m, 0)
+            readouts(m, 0, new_bank(2 * m), new_bank(2 * m + 1))
+        freed = list(range(0, BANKS, 2)) + list(range(1, BANKS, 2))
         for m in range(n_tiles):
-            readouts(m, 1)
-            factor = growth(m)
+            acc, y2, y3 = [new_bank(freed[(3 * m + i) % BANKS]) for i in range(3)]
+            factor = growth(m, acc)
+            readouts(m, 1, y2, y3)
             result = ring.tile([P, PICK], F32, name="result", bufs=4)
             nc.vector.tensor_tensor(out=result[:], in0=y[m][:].indirect(pick[:]), in1=factor[:], op=ALU.mult)
             nc.sync.dma_start(out=out[P * m : P * (m + 1), :], in_=result[:])

@@ -20,13 +20,17 @@ P = 128
 PACK = 4
 PASS = P * PACK
 BANK = 512
+PSUM_BANKS = 8
 QUADS = 4
 QUAD = 32
 ROWS = 4
 LINE = 4
+STRIPE = 16
+WORD = 4
 SLOT = 8192
-BANKS = 8
-ON_VECTOR = {(0, 0): 0, (0, 1): 0, (1, 0): 1, (1, 1): 1}
+HALF_WOVEN = BANK * PACK
+RING = 3
+ON_VECTOR = 1
 
 
 def tile_list_patch_release_features_kernel(
@@ -42,17 +46,29 @@ def tile_list_patch_release_features_kernel(
         keep = ctx.enter_context(tc.tile_pool(name="keep", bufs=1))
         ring = ctx.enter_context(tc.tile_pool(name="ring", bufs=1))
         stage = ctx.enter_context(tc.tile_pool(name="stage", bufs=1))
-        psum = ctx.enter_context(tc.psum_pool(name="psum", bufs=1))
+        psum = ctx.enter_context(tc.psum_pool(name="psum", bufs=PSUM_BANKS))
 
         def kept(shape, dtype, name):
             return keep.tile(shape, dtype, name=name, align_bytes=64)
 
-        idx = keep.tile([P, S // 16], U16, name="idx")
-        idx2 = keep.tile([P, PICK // 16], U16, name="idx2")
-        pick = keep.tile([P, PICK // 16], U16, name="pick")
+        def staged(shape, dtype, name, slot, shift=0):
+            return stage.tile(shape, dtype, name=name, align_bytes=64, offset=SLOT * slot + shift)
 
-        tab_sc = stage.tile([P, T], U8, name="tab_sc", align_bytes=64, offset=SLOT * 6)
-        tab2_sc = stage.tile([P, T3], U8, name="tab2_sc", align_bytes=64, offset=SLOT * 6 + T)
+        def staged_woven(name, slot, shift=0):
+            return staged([P, BANK * PACK], BF16, name, slot, shift)
+
+        def new_woven():
+            return ring.tile([P, BANK * PACK], BF16, name="grouped", bufs=RING, align_bytes=64)
+
+        def new_bank():
+            return psum.tile([P, BANK], F32, name="bank")
+
+        idx = keep.tile([P, S // STRIPE], U16, name="idx")
+        idx2 = keep.tile([P, PICK // STRIPE], U16, name="idx2")
+        pick = keep.tile([P, PICK // STRIPE], U16, name="pick")
+
+        tab_sc = staged([P, T], U8, "tab_sc", 6)
+        tab2_sc = kept([P, T3], U8, "tab2_sc")
         w2_sc = kept([P, r_passes, N], U8, "w2_sc")
         w4_sc = kept([P, m_passes, N], U8, "w4_sc")
         nc.gpsimd.memset(tab_sc[:, : T // 2].bitcast(I32), 0)
@@ -72,8 +88,10 @@ def tile_list_patch_release_features_kernel(
                     in_=src[:, ROWS * q : ROWS * (q + 1), :].rearrange("a r c -> r a c").bitcast(I32),
                 )
 
-        def staged(shape, dtype, name, slot, shift=0):
-            return stage.tile(shape, dtype, name=name, align_bytes=64, offset=SLOT * slot + shift)
+        bias = kept([P, r_passes, PACK], F32, "bias")
+        gains = kept([P, r_passes, PACK], F32, "gains")
+        nc.scalar.dma_start(out=bias[:], in_=b1.rearrange("(b p t) -> p b t", p=P, t=PACK))
+        nc.scalar.dma_start(out=gains[:], in_=gain.rearrange("(b p t) -> p b t", p=P, t=PACK))
 
         def load_rows(src, name, slot):
             raw = staged([P, PACK, BANK], F32, name, slot)
@@ -85,39 +103,39 @@ def tile_list_patch_release_features_kernel(
             nc.sync.dma_start(out=words[:].bitcast(I32), in_=src.rearrange("p t i -> p (t i)").bitcast(I32))
             return words
 
-        def w1_block(a, b):
-            return w1[PASS * a : PASS * (a + 1), PASS * b : PASS * (b + 1)]
+        def load_w1(a, b, slot):
+            block = w1[PASS * a : PASS * (a + 1), PASS * b : PASS * (b + 1)]
+            return load_rows(block, "w1_raw%d%d" % (a, b), slot)
 
-        def quantize(grouped, name):
+        def load_w3(b, slot):
+            return load_rows(w3[PASS * b : PASS * (b + 1), :], "w3_raw%d" % b, slot)
+
+        def quantize(woven, name):
             codes = kept([P, BANK], U32, name + "_codes")
             scales = kept([P, BANK], U8, name + "_scales")
-            nc.vector.quantize_mx(out=codes[:].bitcast(FP8X4), scales=scales[:], in_=grouped[:])
+            nc.vector.quantize_mx(out=codes[:].bitcast(FP8X4), scales=scales[:], in_=woven[:])
             return codes, scales
 
-        def new_rows():
-            return ring.tile([P, PACK, BANK], BF16, name="rows", bufs=3)
-
-        def round_w1(raw, copy, grouped):
+        def round_w1(raw, copy, woven):
             copy(
-                out=grouped[:].rearrange("p (t m j) -> p m j t", t=PACK, j=PACK),
+                out=woven[:].rearrange("p (t m j) -> p m j t", t=PACK, j=PACK),
                 in_=raw[:].rearrange("p j (m t) -> p m j t", t=PACK),
             )
-            return grouped
+            return woven
 
-        def round_w3(raw, copy, grouped):
-            copy(
-                out=grouped[:].rearrange("p (c i j) -> p c j i", i=LINE, j=PACK),
-                in_=raw[:].rearrange("p j (c i) -> p c j i", i=LINE),
+        def weave(rows, woven):
+            nc.vector.tensor_copy(
+                out=woven[:].rearrange("p (c i t) -> p c t i", i=LINE, t=PACK),
+                in_=rows[:].rearrange("p t (c i) -> p c t i", i=LINE),
             )
-            return grouped
+            return woven
 
-        def gather(window, offsets, dtype, name):
-            picked = kept([P, 16 * offsets.shape[1]], dtype, name)
+        def gather(picked, window, offsets):
             nc.vector.tensor_copy(out=picked[:], in_=window[:].indirect(offsets))
             return picked
 
         def idx_half(j):
-            return idx[:, (BANK // 16) * j : (BANK // 16) * (j + 1)]
+            return idx[:, (BANK // STRIPE) * j : (BANK // STRIPE) * (j + 1)]
 
         def mx(acc, lhs, lhs_sc, rhs, rhs_sc, step, steps):
             nc.tensor.matmul_mx(
@@ -125,117 +143,98 @@ def tile_list_patch_release_features_kernel(
                 start=(step == 0), stop=(step == steps - 1),
             )
 
-        def new_bank(n):
-            return psum.tile([P, BANK], F32, name="bank%d" % n)
-
-        w1_raw = {}
-        w1_raw[0, 0] = load_rows(w1_block(0, 0), "w1_raw00", 0)
-        w1_raw[1, 0] = load_rows(w1_block(1, 0), "w1_raw10", 2)
-        tab = [load_words(tab_words[0], T, "tab0", 3)]
-        nc.sync.dma_start(out=idx[:], in_=offs)
-        nc.sync.dma_start(out=idx2[:], in_=offs2)
-        nc.sync.dma_start(out=pick[:], in_=pos1)
-
-        w1_q = {}
-        for a, grouped in enumerate((staged([P, BANK * PACK], BF16, "g00", 1), staged([P, BANK * PACK], BF16, "g10", 8))):
-            w1_q[a, 0] = quantize(round_w1(w1_raw[a, 0], nc.scalar.copy, grouped), "w1_%d0" % a)
-        v_sc = gather(tab_sc, idx[:], U8, "v_sc")
-
-        tab.append(load_words(tab_words[1], T, "tab1", 0))
-        w1_raw[0, 1] = load_rows(w1_block(0, 1), "w1_raw01", 2)
-
-        bias = staged([P, r_passes, PACK], F32, "bias", 8, 512)
-        gains = staged([P, r_passes, PACK], F32, "gains", 8, 576)
-        nc.scalar.dma_start(out=bias[:], in_=b1.rearrange("(b p t) -> p b t", p=P, t=PACK))
-        nc.scalar.dma_start(out=gains[:], in_=gain.rearrange("(b p t) -> p b t", p=P, t=PACK))
-        v = {}
-        tiles = {}
-
         def first_pass(acc, a, b, j, t):
             codes, scales = w1_q[a, b]
             cols = slice(P * t, P * (t + 1))
             mx(acc, codes[:, cols].bitcast(FP8X4), scales[:, cols],
                v[a, j][:].bitcast(FP8X4), v_sc[ROWS * a :, BANK * j : BANK * (j + 1)], a, k_passes)
 
-        def sines(banks, b, j, rows):
-            sine = ring.tile([P, PACK, BANK], F32, name="sine", bufs=3)
+        def sines(four_banks, b):
+            sine = ring.tile([P, PACK, BANK], F32, name="sine", bufs=RING)
+            rows = ring.tile([P, PACK, BANK], BF16, name="rows", bufs=RING)
             for t in range(PACK):
-                nc.scalar.activation(out=sine[:, t, :], in_=banks[t][:], func=ACT.Sin, bias=bias[:, b, t : t + 1])
-            for t in range(ON_VECTOR[b, j], PACK):
+                nc.scalar.activation(out=sine[:, t, :], in_=four_banks[t][:], func=ACT.Sin, bias=bias[:, b, t : t + 1])
+            for t in range(ON_VECTOR, PACK):
                 nc.scalar.activation(out=rows[:, t, :], in_=sine[:, t, :], func=ACT.Copy, scale=gains[:, b, t : t + 1])
             return sine, rows
 
-        def features(b, j, grouped):
-            sine, rows = tiles[b, j]
-            for t in range(ON_VECTOR[b, j]):
+        def features(sine_rows, b, woven):
+            sine, rows = sine_rows
+            for t in range(ON_VECTOR):
                 nc.vector.tensor_scalar_mul(out=rows[:, t, :], in0=sine[:, t, :], scalar1=gains[:, b, t : t + 1])
-            nc.vector.tensor_copy(
-                out=grouped[:].rearrange("p (c i t) -> p c t i", i=LINE, t=PACK),
-                in_=rows[:].rearrange("p t (c i) -> p c t i", i=LINE),
-            )
-            return grouped
+            return weave(rows, woven)
 
-        banks = {}
+        w1_raw, w1_q, v, banks, h_parts, h_q = {}, {}, {}, {}, {}, {}
+        nc.sync.dma_start(out=idx[:], in_=offs)
+        tab = [load_words(tab_words[0], T, "tab0", 0)]
+        w1_raw[0, 0] = load_w1(0, 0, 2)
+        w1_raw[1, 0] = load_w1(1, 0, 3)
+        nc.sync.dma_start(out=idx2[:], in_=offs2)
+        nc.sync.dma_start(out=pick[:], in_=pos1)
+
         for j in range(halves):
-            v[0, j] = gather(tab[0], idx_half(j), U32, "v0%d" % j)
-            banks[j] = [new_bank(PACK * j + t) for t in range(PACK)]
+            v[0, j] = gather(kept([P, BANK], U32, "v0%d" % j), tab[0], idx_half(j))
+        tab.append(load_words(tab_words[1], T, "tab1", 0))
+
+        for a, woven in enumerate((new_woven(), staged_woven("g10", 4))):
+            w1_q[a, 0] = quantize(round_w1(w1_raw[a, 0], nc.scalar.copy, woven), "w1_%d0" % a)
+        v_sc = gather(kept([P, S], U8, "v_sc"), tab_sc, idx[:])
+        w1_raw[0, 1] = load_w1(0, 1, 2)
+
+        for j in range(halves):
+            banks[j] = [new_bank() for t in range(PACK)]
             for t in range(PACK):
                 first_pass(banks[j][t], 0, 0, j, t)
-        v2_sc = staged([P, PICK], U8, "v2_sc", 8)
-        nc.vector.tensor_copy(out=v2_sc[:], in_=tab2_sc[:].indirect(idx2[:]))
-        w1_raw[1, 1] = load_rows(w1_block(1, 1), "w1_raw11", 3)
-        w3_raw = [load_rows(w3[0:PASS, :], "w3_raw0", 4)]
+        w1_raw[1, 1] = load_w1(1, 1, 3)
+        w3_raw = [load_w3(0, 4)]
         for j in range(halves):
-            v[1, j] = stage.tile([P, BANK], U32, name="v1%d" % j, align_bytes=64, offset=SLOT * 6 + T * j)
-            nc.vector.tensor_copy(out=v[1, j][:], in_=tab[1][:].indirect(idx_half(j)))
+            v[1, j] = gather(staged([P, BANK], U32, "v1%d" % j, 6, WORD * BANK * j), tab[1], idx_half(j))
             for t in range(PACK):
                 first_pass(banks[j][t], 1, 0, j, t)
+            h_parts[0, j] = sines(banks[j], 0)
 
-        tiles[0, 0] = sines(banks[0], 0, 0, new_rows())
-        w3_raw.append(load_rows(w3[PASS : 2 * PASS, :], "w3_raw1", 0))
+        w3_raw.append(load_w3(1, 0))
         tab2 = [load_words(tab2_words[0], T3, "tab20", 1)]
-        h_q = {}
-        w1_q[0, 1] = quantize(round_w1(w1_raw[0, 1], nc.vector.tensor_copy, staged([P, BANK * PACK], BF16, "g01", 5)), "w1_01")
+        w1_q[0, 1] = quantize(round_w1(w1_raw[0, 1], nc.vector.tensor_copy, staged_woven("g01", 5)), "w1_01")
         tab2.append(load_words(tab2_words[1], T3, "tab21", 2))
-        w1_g = round_w1(w1_raw[1, 1], nc.vector.tensor_copy, staged([P, BANK * PACK], BF16, "g11", 7, 2048))
-        tab2.append(load_words(tab2_words[2], T3, "tab22", 3))
-        w1_q[1, 1] = quantize(w1_g, "w1_11")
-        tiles[0, 1] = sines(banks[1], 0, 1, staged([P, PACK, BANK], BF16, "rows01", 7, 4096))
-        h00 = features(0, 0, staged([P, BANK * PACK], BF16, "gh00", 7))
-        w3_g = [round_w3(w3_raw[0], nc.vector.tensor_copy, staged([P, BANK * PACK], BF16, "g30", 10))]
-        h_q[0, 0] = quantize(h00, "h00")
-        w3_q = [quantize(w3_g[0], "w3_0")]
-        w2 = staged([P, r_passes, 2 * N], U8, "w2", 10)
+        w2_bytes = r_passes * 2 * N
+        v2_sc = gather(staged([P, PICK], U8, "v2_sc", 5, w2_bytes), tab2_sc, idx2[:])
+        w2 = staged([P, r_passes, 2 * N], U8, "w2", 5)
         nc.sync.dma_start(out=w2[:].bitcast(I32), in_=w2_words.rearrange("a p c -> p a c").bitcast(I32))
+        w1_last = round_w1(w1_raw[1, 1], nc.vector.tensor_copy, staged_woven("g11", 7))
+        tab2.append(load_words(tab2_words[2], T3, "tab22", 3))
+        w1_q[1, 1] = quantize(w1_last, "w1_11")
+
+        woven_h = features(h_parts[0, 0], 0, staged_woven("gh00", 7))
+        woven_w3 = weave(w3_raw[0], new_woven())
+        h_q[0, 0] = quantize(woven_h, "h00")
+        w3_q = [quantize(woven_w3, "w3_0")]
         for j in range(halves):
-            banks[j] = [new_bank(PACK * j + t) for t in range(PACK)]
+            banks[j] = [new_bank() for t in range(PACK)]
             for t in range(PACK):
                 for a in range(k_passes):
                     first_pass(banks[j][t], a, 1, j, t)
-        w3_g.append(round_w3(w3_raw[1], nc.vector.tensor_copy, staged([P, BANK * PACK], BF16, "g31", 11)))
-        h01 = features(0, 1, staged([P, BANK * PACK], BF16, "gh01", 0))
-        w3_q.append(quantize(w3_g[1], "w3_1"))
-        w4 = staged([P, m_passes, N], U32, "w4", 11)
+        woven_h = features(h_parts[0, 1], 0, new_woven())
+        woven_w3 = weave(w3_raw[1], new_woven())
+        w4 = staged([P, m_passes, N], U32, "w4", 4)
         nc.sync.dma_start(out=w4[:].bitcast(I32), in_=w4_words.rearrange("a p c i -> p a (c i)").bitcast(I32))
-        tiles[1, 0] = sines(banks[0], 1, 0, new_rows())
-        tiles[1, 1] = sines(banks[1], 1, 1, stage.tile([P, PACK, BANK], BF16, name="rows11", align_bytes=64, offset=SLOT * 9 + 2048))
-        v2 = [gather(tab2[0], idx2[:], U32, "v20")]
-        h_q[0, 1] = quantize(h01, "h01")
-        v2.append(gather(tab2[1], idx2[:], U32, "v21"))
-        h10 = features(1, 0, staged([P, BANK * PACK], BF16, "gh10", 2, -2048))
-        h_q[1, 0] = quantize(h10, "h10")
-        v2.append(staged([P, PICK], U32, "v22", 2, -2048))
-        nc.vector.tensor_copy(out=v2[2][:], in_=tab2[2][:].indirect(idx2[:]))
-        h11 = features(1, 1, stage.tile([P, BANK * PACK], BF16, name="gh11", align_bytes=64, offset=SLOT * 3 - 2048))
-        h_q[1, 1] = quantize(h11, "h11")
+        for j in range(halves):
+            h_parts[1, j] = sines(banks[j], 1)
+        h_q[0, 1] = quantize(woven_h, "h01")
+        w3_q.append(quantize(woven_w3, "w3_1"))
+        woven_h = features(h_parts[1, 0], 1, new_woven())
+        v2 = [gather(kept([P, PICK], U32, "v20"), tab2[0], idx2[:])]
+        h_q[1, 0] = quantize(woven_h, "h10")
+        for a in range(1, m_passes):
+            v2.append(gather(kept([P, PICK], U32, "v2%d" % a), tab2[a], idx2[:]))
+        woven_h = features(h_parts[1, 1], 1, staged_woven("gh11", 3, -HALF_WOVEN))
+        h_q[1, 1] = quantize(woven_h, "h11")
 
-        y = [
-            stage.tile([P, S], F32, name="y%d" % m, align_bytes=64, offset=offset)
-            for m, offset in enumerate((SLOT * 3 - 4096, SLOT * 3, SLOT * 9, SLOT * 9 + 4096))
-        ]
+        y = [kept([P, S], F32, "y%d" % m) for m in range(n_tiles)]
 
-        def readouts(m, j, y2, y3):
+        def readouts(m, j):
             cols = slice(P * m, P * (m + 1))
+            y2, y3 = new_bank(), new_bank()
             for b in range(r_passes):
                 codes, scales = h_q[b, j]
                 mx(y2, w2[:, b, 2 * P * m : 2 * P * (m + 1)].bitcast(FP4X4), w2_sc[:, b, cols],
@@ -245,12 +244,13 @@ def tile_list_patch_release_features_kernel(
                 w_codes, w_scales = w3_q[b]
                 mx(y3, w_codes[:, cols].bitcast(FP8X4), w_scales[:, cols],
                    codes[:].bitcast(FP8X4), scales[:], b, r_passes)
-            y2_sb = ring.tile([P, BANK], F32, name="y2_sb", bufs=3)
+            y2_sb = ring.tile([P, BANK], F32, name="y2_sb", bufs=RING)
             nc.scalar.copy(out=y2_sb[:], in_=y2[:])
             nc.vector.tensor_tensor(out=y[m][:, BANK * j : BANK * (j + 1)], in0=y3[:], in1=y2_sb[:], op=ALU.min)
 
-        def growth(m, acc):
+        def growth(m):
             cols = slice(P * m, P * (m + 1))
+            acc = new_bank()
             for a in range(m_passes):
                 mx(acc, w4[:, a, cols].bitcast(FP8X4), w4_sc[:, a, cols],
                    v2[a][:].bitcast(FP8X4), v2_sc[ROWS * a :, :], a, m_passes)
@@ -259,12 +259,10 @@ def tile_list_patch_release_features_kernel(
             return factor
 
         for m in range(n_tiles):
-            readouts(m, 0, new_bank(2 * m), new_bank(2 * m + 1))
-        freed = list(range(0, BANKS, 2)) + list(range(1, BANKS, 2))
+            readouts(m, 0)
         for m in range(n_tiles):
-            acc, y2, y3 = [new_bank(freed[(3 * m + i) % BANKS]) for i in range(3)]
-            factor = growth(m, acc)
-            readouts(m, 1, y2, y3)
-            result = ring.tile([P, PICK], F32, name="result", bufs=4)
+            readouts(m, 1)
+            factor = growth(m)
+            result = ring.tile([P, PICK], F32, name="result", bufs=n_tiles)
             nc.vector.tensor_tensor(out=result[:], in0=y[m][:].indirect(pick[:]), in1=factor[:], op=ALU.mult)
             nc.sync.dma_start(out=out[P * m : P * (m + 1), :], in_=result[:])

from contextlib import ExitStack

import concourse.mybir as mybir

K, H, N, K2, T, T3, S, PICK = 1024, 1024, 512, 1536, 4096, 2048, 1024, 512
FLOPS = 2 * (K * H * S + 2 * H * N * S + K2 * N * PICK)

F32 = mybir.dt.float32
BF16 = mybir.dt.bfloat16
I32 = mybir.dt.int32
U32 = mybir.dt.uint32
U16 = mybir.dt.uint16
U8 = mybir.dt.uint8
FP8X4 = mybir.dt.float8_e4m3fn_x4
FP4X4 = mybir.dt.float4_e2m1fn_x4
ACT = mybir.ActivationFunctionType
ALU = mybir.AluOpType

P = 128
PACK = 4
PASS = P * PACK
BANK = 512
PSUM_BANKS = 8
QUADS = 4
QUAD = 32
ROWS = 4
LINE = 4
STRIPE = 16
WORD = 4
SLOT = 8192
HALF_WOVEN = BANK * PACK
RING = 3
ON_VECTOR = 1


def tile_list_patch_release_features_kernel(
    tc, tab_words, tab_scales, offs, tab2_words, tab2_scales, offs2, pos1,
    w1, b1, gain, w2_words, w2_scales, w3, w4_words, w4_scales, out,
):
    nc = tc.nc
    k_passes, r_passes, m_passes = K // PASS, H // PASS, K2 // PASS
    halves = S // BANK
    n_tiles = N // P

    with ExitStack() as ctx:
        keep = ctx.enter_context(tc.tile_pool(name="keep", bufs=1))
        ring = ctx.enter_context(tc.tile_pool(name="ring", bufs=1))
        stage = ctx.enter_context(tc.tile_pool(name="stage", bufs=1))
        psum = ctx.enter_context(tc.psum_pool(name="psum", bufs=PSUM_BANKS))

        def kept(shape, dtype, name):
            return keep.tile(shape, dtype, name=name, align_bytes=64)

        def staged(shape, dtype, name, slot, shift=0):
            return stage.tile(shape, dtype, name=name, align_bytes=64, offset=SLOT * slot + shift)

        def staged_woven(name, slot, shift=0):
            return staged([P, BANK * PACK], BF16, name, slot, shift)

        def new_woven():
            return ring.tile([P, BANK * PACK], BF16, name="grouped", bufs=RING, align_bytes=64)

        def new_bank():
            return psum.tile([P, BANK], F32, name="bank")

        idx = keep.tile([P, S // STRIPE], U16, name="idx")
        idx2 = keep.tile([P, PICK // STRIPE], U16, name="idx2")
        pick = keep.tile([P, PICK // STRIPE], U16, name="pick")

        tab_sc = staged([P, T], U8, "tab_sc", 6)
        tab2_sc = kept([P, T3], U8, "tab2_sc")
        w2_sc = kept([P, r_passes, N], U8, "w2_sc")
        w4_sc = kept([P, m_passes, N], U8, "w4_sc")
        nc.gpsimd.memset(tab_sc[:, : T // 2].bitcast(I32), 0)
        nc.vector.memset(tab_sc[:, T // 2 :].bitcast(I32), 0)
        for plane in (tab2_sc[:], w2_sc[:], w4_sc[:]):
            nc.vector.memset(plane.bitcast(I32), 0)
        for plane, src, passes in ((tab_sc, tab_scales, k_passes), (tab2_sc, tab2_scales, m_passes)):
            for q in range(QUADS):
                nc.gpsimd.dma_start(
                    out=plane[QUAD * q : QUAD * q + ROWS * passes, :].bitcast(I32),
                    in_=src[:, ROWS * q : ROWS * (q + 1), :].bitcast(I32),
                )
        for plane, src in ((w2_sc, w2_scales), (w4_sc, w4_scales)):
            for q in range(QUADS):
                nc.gpsimd.dma_start(
                    out=plane[QUAD * q : QUAD * q + ROWS, :, :].bitcast(I32),
                    in_=src[:, ROWS * q : ROWS * (q + 1), :].rearrange("a r c -> r a c").bitcast(I32),
                )

        bias = kept([P, r_passes, PACK], F32, "bias")
        gains = kept([P, r_passes, PACK], F32, "gains")
        nc.scalar.dma_start(out=bias[:], in_=b1.rearrange("(b p t) -> p b t", p=P, t=PACK))
        nc.scalar.dma_start(out=gains[:], in_=gain.rearrange("(b p t) -> p b t", p=P, t=PACK))

        def load_rows(src, name, slot):
            raw = staged([P, PACK, BANK], F32, name, slot)
            nc.sync.dma_start(out=raw[:], in_=src.rearrange("(p j) c -> p j c", j=PACK))
            return raw

        def load_words(src, width, name, slot):
            words = staged([P, width], U32, name, slot)
            nc.sync.dma_start(out=words[:].bitcast(I32), in_=src.rearrange("p t i -> p (t i)").bitcast(I32))
            return words

        def load_w1(a, b, slot):
            block = w1[PASS * a : PASS * (a + 1), PASS * b : PASS * (b + 1)]
            return load_rows(block, "w1_raw%d%d" % (a, b), slot)

        def load_w3(b, slot):
            return load_rows(w3[PASS * b : PASS * (b + 1), :], "w3_raw%d" % b, slot)

        def quantize(woven, name):
            codes = kept([P, BANK], U32, name + "_codes")
            scales = kept([P, BANK], U8, name + "_scales")
            nc.vector.quantize_mx(out=codes[:].bitcast(FP8X4), scales=scales[:], in_=woven[:])
            return codes, scales

        def round_w1(raw, copy, woven):
            copy(
                out=woven[:].rearrange("p (t m j) -> p m j t", t=PACK, j=PACK),
                in_=raw[:].rearrange("p j (m t) -> p m j t", t=PACK),
            )
            return woven

        def weave(rows, woven):
            nc.vector.tensor_copy(
                out=woven[:].rearrange("p (c i t) -> p c t i", i=LINE, t=PACK),
                in_=rows[:].rearrange("p t (c i) -> p c t i", i=LINE),
            )
            return woven

        def gather(picked, window, offsets):
            nc.vector.tensor_copy(out=picked[:], in_=window[:].indirect(offsets))
            return picked

        def idx_half(j):
            return idx[:, (BANK // STRIPE) * j : (BANK // STRIPE) * (j + 1)]

        def mx(acc, lhs, lhs_sc, rhs, rhs_sc, step, steps):
            nc.tensor.matmul_mx(
                out=acc[:], lhsT=lhs, lhsT_scale=lhs_sc, rhs=rhs, rhs_scale=rhs_sc,
                start=(step == 0), stop=(step == steps - 1),
            )

        def first_pass(acc, a, b, j, t):
            codes, scales = w1_q[a, b]
            cols = slice(P * t, P * (t + 1))
            mx(acc, codes[:, cols].bitcast(FP8X4), scales[:, cols],
               v[a, j][:].bitcast(FP8X4), v_sc[ROWS * a :, BANK * j : BANK * (j + 1)], a, k_passes)

        def sines(four_banks, b):
            sine = ring.tile([P, PACK, BANK], F32, name="sine", bufs=RING)
            rows = ring.tile([P, PACK, BANK], BF16, name="rows", bufs=RING)
            for t in range(PACK):
                nc.scalar.activation(out=sine[:, t, :], in_=four_banks[t][:], func=ACT.Sin, bias=bias[:, b, t : t + 1])
            for t in range(ON_VECTOR, PACK):
                nc.scalar.activation(out=rows[:, t, :], in_=sine[:, t, :], func=ACT.Copy, scale=gains[:, b, t : t + 1])
            return sine, rows

        def features(sine_rows, b, woven):
            sine, rows = sine_rows
            for t in range(ON_VECTOR):
                nc.vector.tensor_scalar_mul(out=rows[:, t, :], in0=sine[:, t, :], scalar1=gains[:, b, t : t + 1])
            return weave(rows, woven)

        w1_raw, w1_q, v, banks, h_parts, h_q = {}, {}, {}, {}, {}, {}
        nc.sync.dma_start(out=idx[:], in_=offs)
        tab = [load_words(tab_words[0], T, "tab0", 0)]
        w1_raw[0, 0] = load_w1(0, 0, 2)
        w1_raw[1, 0] = load_w1(1, 0, 3)
        nc.sync.dma_start(out=idx2[:], in_=offs2)
        nc.sync.dma_start(out=pick[:], in_=pos1)

        for j in range(halves):
            v[0, j] = gather(kept([P, BANK], U32, "v0%d" % j), tab[0], idx_half(j))
        tab.append(load_words(tab_words[1], T, "tab1", 0))

        for a, woven in enumerate((new_woven(), staged_woven("g10", 4))):
            w1_q[a, 0] = quantize(round_w1(w1_raw[a, 0], nc.scalar.copy, woven), "w1_%d0" % a)
        v_sc = gather(kept([P, S], U8, "v_sc"), tab_sc, idx[:])
        w1_raw[0, 1] = load_w1(0, 1, 2)

        for j in range(halves):
            banks[j] = [new_bank() for t in range(PACK)]
            for t in range(PACK):
                first_pass(banks[j][t], 0, 0, j, t)
        w1_raw[1, 1] = load_w1(1, 1, 3)
        w3_raw = [load_w3(0, 4)]
        for j in range(halves):
            v[1, j] = gather(staged([P, BANK], U32, "v1%d" % j, 6, WORD * BANK * j), tab[1], idx_half(j))
            for t in range(PACK):
                first_pass(banks[j][t], 1, 0, j, t)
            h_parts[0, j] = sines(banks[j], 0)

        w3_raw.append(load_w3(1, 0))
        tab2 = [load_words(tab2_words[0], T3, "tab20", 1)]
        w1_q[0, 1] = quantize(round_w1(w1_raw[0, 1], nc.vector.tensor_copy, staged_woven("g01", 5)), "w1_01")
        tab2.append(load_words(tab2_words[1], T3, "tab21", 2))
        w2_bytes = r_passes * 2 * N
        v2_sc = gather(staged([P, PICK], U8, "v2_sc", 5, w2_bytes), tab2_sc, idx2[:])
        w2 = staged([P, r_passes, 2 * N], U8, "w2", 5)
        nc.sync.dma_start(out=w2[:].bitcast(I32), in_=w2_words.rearrange("a p c -> p a c").bitcast(I32))
        w1_last = round_w1(w1_raw[1, 1], nc.vector.tensor_copy, staged_woven("g11", 7))
        tab2.append(load_words(tab2_words[2], T3, "tab22", 3))
        w1_q[1, 1] = quantize(w1_last, "w1_11")

        woven_h = features(h_parts[0, 0], 0, staged_woven("gh00", 7))
        woven_w3 = weave(w3_raw[0], new_woven())
        h_q[0, 0] = quantize(woven_h, "h00")
        w3_q = [quantize(woven_w3, "w3_0")]
        for j in range(halves):
            banks[j] = [new_bank() for t in range(PACK)]
            for t in range(PACK):
                for a in range(k_passes):
                    first_pass(banks[j][t], a, 1, j, t)
        woven_h = features(h_parts[0, 1], 0, new_woven())
        woven_w3 = weave(w3_raw[1], new_woven())
        w4 = staged([P, m_passes, N], U32, "w4", 4)
        nc.sync.dma_start(out=w4[:].bitcast(I32), in_=w4_words.rearrange("a p c i -> p a (c i)").bitcast(I32))
        for j in range(halves):
            h_parts[1, j] = sines(banks[j], 1)
        h_q[0, 1] = quantize(woven_h, "h01")
        w3_q.append(quantize(woven_w3, "w3_1"))
        woven_h = features(h_parts[1, 0], 1, new_woven())
        v2 = [gather(kept([P, PICK], U32, "v20"), tab2[0], idx2[:])]
        h_q[1, 0] = quantize(woven_h, "h10")
        for a in range(1, m_passes):
            v2.append(gather(kept([P, PICK], U32, "v2%d" % a), tab2[a], idx2[:]))
        woven_h = features(h_parts[1, 1], 1, staged_woven("gh11", 3, -HALF_WOVEN))
        h_q[1, 1] = quantize(woven_h, "h11")

        y = [kept([P, S], F32, "y%d" % m) for m in range(n_tiles)]

        def readouts(m, j):
            cols = slice(P * m, P * (m + 1))
            y2, y3 = new_bank(), new_bank()
            for b in range(r_passes):
                codes, scales = h_q[b, j]
                mx(y2, w2[:, b, 2 * P * m : 2 * P * (m + 1)].bitcast(FP4X4), w2_sc[:, b, cols],
                   codes[:].bitcast(FP8X4), scales[:], b, r_passes)
            for b in range(r_passes):
                codes, scales = h_q[b, j]
                w_codes, w_scales = w3_q[b]
                mx(y3, w_codes[:, cols].bitcast(FP8X4), w_scales[:, cols],
                   codes[:].bitcast(FP8X4), scales[:], b, r_passes)
            y2_sb = ring.tile([P, BANK], F32, name="y2_sb", bufs=RING)
            nc.scalar.copy(out=y2_sb[:], in_=y2[:])
            nc.vector.tensor_tensor(out=y[m][:, BANK * j : BANK * (j + 1)], in0=y3[:], in1=y2_sb[:], op=ALU.min)

        def growth(m):
            cols = slice(P * m, P * (m + 1))
            acc = new_bank()
            for a in range(m_passes):
                mx(acc, w4[:, a, cols].bitcast(FP8X4), w4_sc[:, a, cols],
                   v2[a][:].bitcast(FP8X4), v2_sc[ROWS * a :, :], a, m_passes)
            factor = kept([P, PICK], F32, "factor%d" % m)
            nc.scalar.activation(out=factor[:], in_=acc[:], func=ACT.Exp)
            return factor

        for m in range(n_tiles):
            readouts(m, 0)
        for m in range(n_tiles):
            readouts(m, 1)
            factor = growth(m)
            result = ring.tile([P, PICK], F32, name="result", bufs=n_tiles)
            nc.vector.tensor_tensor(out=result[:], in0=y[m][:].indirect(pick[:]), in1=factor[:], op=ALU.mult)
            nc.sync.dma_start(out=out[P * m : P * (m + 1), :], in_=result[:])
